import numpy as np, ml_dtypes
CORES = [37,45,53,61,69,109,117,125]
N = 8
NH, QP = 4, 64
def setup_inputs(rng):
    q = rng.standard_normal((N, 128, NH * QP), dtype=np.float32) / 4; k = rng.standard_normal((N, 128, NH * 128), dtype=np.float32)
    a = 2 * np.pi * rng.random((N, NH * QP)); s = 400 * rng.random((N, NH * QP)) ** 1.5; q[:, 0, :] = s * np.cos(a); q[:, 1, :] = s * np.sin(a); q[:, 2, :] = 150 * rng.standard_normal((N, NH * QP)); k[:, 2, :] = 1 + k[:, 2, :] / 50
    a = (2 * np.pi * rng.random((1, NH, 1)) + np.pi / 2 * (rng.permuted(np.tile(np.arange(N), (NH, 1)), axis=1).T.reshape(N, NH, 1) + 0.5) / N - 0.5 + rng.random((N, NH, 128))).reshape(N, NH * 128); k[:, 0, :] = np.cos(a); k[:, 1, :] = np.sin(a)
    return {"q": q.astype(ml_dtypes.bfloat16), "k": k.astype(ml_dtypes.bfloat16), "v": rng.standard_normal((N, 128, NH * 128), dtype=np.float32).astype(ml_dtypes.bfloat16)}
def setup_inputs_big(rng):
    d = setup_inputs(rng)
    for k in ("v",): d[k] = (d[k].astype(np.float32) * 1048576.0).astype(d[k].dtype)
    return d
def setup_inputs_small(rng):
    d = setup_inputs(rng)
    for k in ("v",): d[k] = (d[k].astype(np.float32) * (1 / 1048576.0)).astype(d[k].dtype)
    return d
def reference(q, k, v):
    Q, K, V = q.astype(np.float64), k.astype(np.float64), v.astype(np.float64)
    y = np.zeros((N, QP, NH * 128))
    for r in range(N):
        for h in range(NH):
            S = np.concatenate([K[j][:, 128 * h:128 * h + 128].T @ Q[r][:, QP * h:QP * h + QP] for j in range(N)], axis=0)
            P = np.exp(S - S.max(axis=0)); P = P / P.sum(axis=0)
            y[r][:, 128 * h:128 * h + 128] = P.T @ np.concatenate([V[j][:, 128 * h:128 * h + 128] for j in range(N)], axis=0)
    return {"y": y.astype(ml_dtypes.bfloat16)}

@@ -1,0 +1,277 @@
+from concourse.bass import DstId, RemoteDMATransfer
+from concourse.mybir import AluOpType, AxisListType, ActivationFunctionType
+
+NH, QP, KP = 4, 64, 128
+PW = KP + KP + QP
+OW = 130
+OS = 136
+
+SCRATCH = {
+    "qs": ("sbuf", [128, NH * QP], "bfloat16"),
+    "stage": ("sbuf", [128, NH * PW], "bfloat16"),
+    "res": ("sbuf", [128, 2 * NH * OS], "bfloat16"),
+    "sm": ("sbuf", [128, NH * 8], "float32"),
+    "tb": ("sbuf", [128, NH * 128], "float32"),
+    "ysb": ("sbuf", [128, NH * 128], "bfloat16"),
+    "qrel": ("sbuf", [128, NH * QP], "bfloat16"),
+    "land": ("sbuf", [128, 4 * PW], "bfloat16"),
+    "qx": ("sbuf", [128, 4 * QP], "bfloat16"),
+    "ones": ("sbuf", [128, 128], "bfloat16"),
+    "ident": ("sbuf", [128, 128], "bfloat16"),
+    "pw": ("sbuf", [128, 4 * 512], "bfloat16"),
+    "pk": ("sbuf", [128, 4 * 512], "bfloat16"),
+    "lacc": ("sbuf", [128, 4], "float32"),
+    "ob": ("sbuf", [128, 4 * OS], "bfloat16"),
+    "ps0": ("psum", [128, 512], "float32"),
+    "ps1": ("psum", [128, 512], "float32"),
+    "ps2": ("psum", [128, 512], "float32"),
+    "ps3": ("psum", [128, 512], "float32"),
+    "pt0": ("psum", [128, 1024], "bfloat16"),
+    "pt1": ("psum", [128, 1024], "bfloat16"),
+    "po0": ("psum", [128, 512], "float32"),
+    "po1": ("psum", [128, 512], "float32"),
+}
+SEMAPHORES = (["ldq", "qr", "snt", "st", "id0", "id1", "qx0", "qx1"]
+              + ["%s%d" % (n, i) for n in ("ld", "kv", "rs", "ch", "sS", "sM", "sE", "sT", "sC", "sL", "sO", "sV")
+                 for i in range(4)])
+
+Exp = ActivationFunctionType.Exp
+Copy = ActivationFunctionType.Copy
+
+
+def _bits(m):
+    return [1 << e for e in range(m.bit_length()) if (m >> e) & 1]
+
+
+def _join(bs):
+    m = 0
+    for b in bs:
+        m |= b
+    return m
+
+
+def _plan(T, topo):
+    cores = list(T.cores)
+    c0 = topo.chip(cores[0])
+    cls = [[], []]
+    for r, c in enumerate(cores):
+        ch = topo.chip(c)
+        cls[0 if (ch == c0 or topo.same_plane(ch, c0)) else 1].append(r)
+    work = [[None] * NH, [None] * NH]
+    for p in range(2):
+        for h in range(NH):
+            rc = cores[cls[p][h]]
+            cand = [c for c in range(topo.CHIPS * topo.CORES_PER_CHIP)
+                    if topo.chip(c) == topo.chip(rc) and c not in cores and topo.die(c) == topo.die(rc)
+                    and all(topo.may_write(c, d) for d in cores)]
+            work[p][h] = cand[0]
+    return cores, cls, work
+
+
+def _offs(s):
+    return (KP, 0, 2 * KP) if s % 2 == 0 else (QP, QP + KP, 0)
+
+
+def _rank(g, core, T, topo, cores, cls, work, p, s):
+    S = T.sem
+    ko, vo, qo = _offs(s)
+    mine = work[p][s]
+    away = [work[p][h] for h in range(NH) if h != s]
+    m_off = topo.mask(core, away[0])
+    m_on = _join([b for b in _bits(topo.mask(core, mine)) if not (b & m_off)])
+    order = [(s + 1 + i) % NH for i in range(NH)]
+    g.sync.dma_start(T.qs[:, :], T.q[:, :]).then_inc(S.ldq, 16)
+    for n, h in enumerate(order):
+        b = PW * h
+        g.sync.dma_start(T.stage[:, b + ko:b + ko + KP], T.k[:, KP * h:KP * h + KP]).then_inc(S["ld%d" % h], 16)
+        g.scalar.dma_start(T.stage[:, b + vo:b + vo + KP], T.v[:, KP * h:KP * h + KP]).then_inc(S["ld%d" % h], 16)
+        qq = g.sync if n % 2 else g.scalar
+        qq.dma_start(T.stage[:, b + qo:b + qo + QP], T.q[:, QP * h:QP * h + QP]).then_inc(S["ld%d" % h], 16)
+    sent = 0
+    rid, pid, _ = topo.addr(mine)
+    g.wait_ge(S.ldq, 16)
+    g.remote_dma(T.qrel[:, :], T.qs[:, :], S.qr, S.snt, pid, rid, m_on)
+    sent += len(_bits(m_on))
+    for h in order:
+        dst = work[p][h]
+        m = m_on if dst == mine else m_off
+        rid, pid, _ = topo.addr(dst)
+        g.wait_ge(S["ld%d" % h], 48)
+        g.remote_dma(T.land[:, PW * s:PW * s + PW], T.stage[:, PW * h:PW * h + PW], S["kv%d" % s], S.snt, pid, rid, m)
+        sent += len(_bits(m))
+    g.wait_ge(S.snt, sent)
+    tile = 2 * p + s // 2
+    lo = 64 * (s % 2)
+    hi = lo + 64
+    V, A = g.vector, g.scalar
+    for i in range(NH):
+        h = (tile - i) % NH
+        ch, rs = S["ch%d" % h], S["rs%d" % h]
+        a0, b0 = (2 * h) * OS, (2 * h + 1) * OS
+        sm = 8 * h
+        ps = T["ps%d" % h]
+
+        def col(c):
+            return T.sm[lo:hi, sm + c:sm + c + 1]
+        V.wait_ge(rs, 8)
+        A.wait_ge(rs, 8)
+        V.tensor_tensor(col(0), T.res[lo:hi, a0 + 129:a0 + 130], T.res[lo:hi, b0 + 129:b0 + 130],
+                        AluOpType.min).then_inc(ch, 1)
+        A.wait_ge(ch, 1)
+        A.activation(col(1), T.res[lo:hi, a0 + 129:a0 + 130], Exp, bias=col(0), scale=-1.0).then_inc(ch, 1)
+        A.activation(col(2), T.res[lo:hi, b0 + 129:b0 + 130], Exp, bias=col(0), scale=-1.0).then_inc(ch, 1)
+        V.wait_ge(ch, 3)
+        V.tensor_scalar(col(3), T.res[lo:hi, a0 + 128:a0 + 129], col(1), None, AluOpType.mult).then_inc(ch, 1)
+        V.wait_ge(ch, 4)
+        V.tensor_scalar(col(4), T.res[lo:hi, b0 + 128:b0 + 129], col(2), col(3),
+                        AluOpType.mult, AluOpType.add).then_inc(ch, 1)
+        V.wait_ge(ch, 5)
+        V.reciprocal(col(5), col(4)).then_inc(ch, 1)
+        V.wait_ge(ch, 6)
+        V.tensor_scalar(T.sm[lo:hi, sm + 6:sm + 8], T.sm[lo:hi, sm + 1:sm + 3], col(5), None,
+                        AluOpType.mult).then_inc(ch, 1)
+        A.wait_ge(ch, 7)
+        V.wait_ge(ch, 7)
+        A.activation(ps[lo:hi, 0:128], T.res[lo:hi, a0:a0 + 128], Copy, scale=col(6)).then_inc(ch, 1)
+        V.tensor_scalar(T.tb[lo:hi, 128 * h:128 * h + 128], T.res[lo:hi, b0:b0 + 128], col(7), None,
+                        AluOpType.mult).then_inc(ch, 1)
+        V.wait_ge(ch, 9)
+        V.tensor_tensor(T.ysb[lo:hi, 128 * h:128 * h + 128], ps[lo:hi, 0:128], T.tb[lo:hi, 128 * h:128 * h + 128],
+                        AluOpType.add).then_inc(ch, 1)
+        g.sync.wait_ge(ch, 10)
+        g.sync.dma_start(T.y[:, 128 * h:128 * h + 128], T.ysb[lo:hi, 128 * h:128 * h + 128]).then_inc(S.st, 16)
+    g.sync.wait_ge(S.st, 16 * NH)
+
+
+def _worker(g, core, T, topo, cores, cls, work, p, h):
+    S = T.sem
+    P, V, A = g.tensor, g.vector, g.scalar
+    V.memset(T.ones[:, :], 1.0).then_inc(S.id0, 1)
+    g.wait_ge(S.id0, 1)
+    g.affine_select(T.ident[:, :], T.ones[:, :], [[-1, 128]], AluOpType.is_equal, 0.0, 0, 1).then_inc(S.id1, 1)
+    sent = 0
+    far = [work[1 - p][hh] for hh in range(NH)]
+    eb = _bits(_join([0]) | topo.mask(core, far[0]))
+    per = len(eb) // NH
+    g.wait_ge(S.qr, len(_bits(topo.mask(cores[cls[p][h]], core))) - len(eb))
+    trs = []
+    for hh in range(NH):
+        rid, pid, _ = topo.addr(far[hh])
+        trs.append(RemoteDMATransfer(dst_ids=[DstId(rid=rid, pnc=pid)], dma_engine_mask=_join(eb[per * hh:per * hh + per]),
+                                     remote_sem=S["qx%d" % (h // 2)], src=T.qrel[:, QP * hh:QP * hh + QP],
+                                     dst=T.qx[:, QP * h:QP * h + QP]))
+        sent += per
+    g.remote_dma_fused(trs, local_sem=S.snt)
+
+    tiles = [(h + i) % 4 for i in range(4)]
+
+    def qtile(t):
+        c, a = t // 2, t % 2
+        if c == p:
+            return T.land[:, 2 * PW * a + 2 * KP:2 * PW * a + 2 * KP + 2 * QP]
+        return T.qx[:, 2 * QP * a:2 * QP * a + 2 * QP]
+
+    def kblk(j):
+        o = PW * j + _offs(j)[0]
+        return T.land[:, o:o + KP]
+
+    def vblk(j):
+        o = PW * j + _offs(j)[1]
+        return T.land[:, o:o + KP]
+    ps = [T["ps%d" % i] for i in range(4)]
+    pt = [T.pt0, T.pt1]
+    po = [T.po0, T.po1]
+    n_off = len(eb)
+    arr = [(h - 1 - i) % 4 for i in range(4)]
+    events = [("k", arr[0]), ("x", 0), ("x", 1), ("k", arr[1]), ("k", arr[2]), ("k", arr[3])]
+    havek, havex, done = [], [], []
+    for kind, n in events:
+        if kind == "k":
+            P.wait_ge(S["kv%d" % n], n_off)
+            havek.append(n)
+        else:
+            P.wait_ge(S["qx%d" % n], 2 * per)
+            havex.append(n)
+        for i, t in enumerate(tiles):
+            c, a = t // 2, t % 2
+            ok = (2 * a in havek and 2 * a + 1 in havek) if c == p else (a in havex)
+            if not ok:
+                continue
+            for j in havek:
+                if (i, j) in done:
+                    continue
+                done.append((i, j))
+                P.matmul(ps[i][:, KP * j:KP * j + KP], qtile(t), kblk(j), True, True).then_inc(S["sS%d" % i], 1)
+
+    def nmcol(i):
+        return T.ob[:, OS * i + 129:OS * i + 130]
+
+    def v_max(i):
+        V.wait_ge(S["sS%d" % i], 4)
+        V.tensor_reduce(nmcol(i), ps[i][:, :], AxisListType.X, AluOpType.max, negate=True).then_inc(S["sM%d" % i], 1)
+
+    def a_exp(i):
+        A.wait_ge(S["sM%d" % i], 1)
+        A.activation(T.pw[:, 512 * i:512 * i + 512], ps[i][:, :], Exp, bias=nmcol(i),
+                     accum_out=T.lacc[:, i:i + 1]).then_inc(S["sE%d" % i], 1)
+
+    def p_tr(i):
+        P.wait_ge(S["sE%d" % i], 1)
+        if i >= 2:
+            P.wait_ge(S["sC%d" % (i - 2)], 1)
+        for j in range(4):
+            P.transpose(pt[i % 2][:, 128 * j:128 * j + 128], T.pw[:, 512 * i + 128 * j:512 * i + 128 * j + 128],
+                        T.ident[:, :]).then_inc(S["sT%d" % i], 1)
+
+    def v_cp(i):
+        V.wait_ge(S["sT%d" % i], 4)
+        V.tensor_copy(T.pk[:, 512 * i:512 * i + 512], pt[i % 2][:, 0:512]).then_inc(S["sC%d" % i], 1)
+        V.tensor_copy(T.ob[:, OS * i + 128:OS * i + 129], T.lacc[:, i:i + 1]).then_inc(S["sL%d" % i], 1)
+
+    def p_pv(i):
+        P.wait_ge(S["sC%d" % i], 1)
+        if i >= 2:
+            P.wait_ge(S["sV%d" % (i - 2)], 1)
+        for j in range(4):
+            P.matmul(po[i % 2][:, 0:128], T.pk[:, 512 * i + 128 * j:512 * i + 128 * j + 128], vblk(j),
+                     j == 0, j == 3).then_inc(S["sO%d" % i], 1)
+
+    def a_ev(i):
+        A.wait_ge(S["sO%d" % i], 4)
+        A.activation(T.ob[:, OS * i:OS * i + 128], po[i % 2][:, 0:128], Copy).then_inc(S["sV%d" % i], 1)
+
+    for f, i in ((v_max, 0), (v_max, 1), (v_max, 2), (v_cp, 0), (v_max, 3), (v_cp, 1), (v_cp, 2), (v_cp, 3)):
+        f(i)
+    for f, i in ((a_exp, 0), (a_exp, 1), (a_exp, 2), (a_ev, 0), (a_exp, 3), (a_ev, 1), (a_ev, 2), (a_ev, 3)):
+        f(i)
+    P.wait_ge(S.id1, 1)
+    for f, i in ((p_tr, 0), (p_tr, 1), (p_pv, 0), (p_tr, 2), (p_pv, 1), (p_tr, 3), (p_pv, 2), (p_pv, 3)):
+        f(i)
+    slot = (2 * h + p) * OS
+    for i, t in enumerate(tiles):
+        c, a = t // 2, t % 2
+        dsts = [cores[cls[c][2 * a]], cores[cls[c][2 * a + 1]]]
+        bs = _bits(topo.mask(core, dsts[0]) & topo.mask(core, dsts[1]) & _join(eb))
+        half = len(bs) // 2
+        g.wait_ge(S["sV%d" % i], 1)
+        g.wait_ge(S["sL%d" % i], 1)
+        trs = []
+        for n, d in enumerate(dsts):
+            rid, pid, _ = topo.addr(d)
+            trs.append(RemoteDMATransfer(dst_ids=[DstId(rid=rid, pnc=pid)],
+                                         dma_engine_mask=_join(bs[half * n:half * n + half]),
+                                         remote_sem=S["rs%d" % h], src=T.ob[:, OS * i:OS * i + OW],
+                                         dst=T.res[:, slot:slot + OW]))
+            sent += half
+        g.remote_dma_fused(trs, local_sem=S.snt)
+    g.wait_ge(S.snt, sent)
+
+
+def rank_program(g, core, T, topo):
+    cores, cls, work = _plan(T, topo)
+    for p in range(2):
+        for n in range(NH):
+            if cores[cls[p][n]] == core:
+                _rank(g, core, T, topo, cores, cls, work, p, n)
+            if work[p][n] == core:
+                _worker(g, core, T, topo, cores, cls, work, p, n)

@@ -4,15 +4,11 @@ from concourse.mybir import AluOpType, AxisListType, ActivationFunctionType
 NH, QP, KP = 4, 64, 128
 PW = KP + KP + QP
 OW = 130
-OS = 136
 
 SCRATCH = {
     "qs": ("sbuf", [128, NH * QP], "bfloat16"),
     "stage": ("sbuf", [128, NH * PW], "bfloat16"),
-    "res": ("sbuf", [128, 2 * NH * OS], "bfloat16"),
-    "sm": ("sbuf", [128, NH * 8], "float32"),
-    "tb": ("sbuf", [128, NH * 128], "float32"),
-    "ysb": ("sbuf", [128, NH * 128], "bfloat16"),
+    "res": ("sbuf", [128, NH * 128], "bfloat16"),
     "qrel": ("sbuf", [128, NH * QP], "bfloat16"),
     "land": ("sbuf", [128, 4 * PW], "bfloat16"),
     "qx": ("sbuf", [128, 4 * QP], "bfloat16"),
@@ -21,18 +17,23 @@ SCRATCH = {
     "pw": ("sbuf", [128, 4 * 512], "bfloat16"),
     "pk": ("sbuf", [128, 4 * 512], "bfloat16"),
     "lacc": ("sbuf", [128, 4], "float32"),
-    "ob": ("sbuf", [128, 4 * OS], "bfloat16"),
+    "ob": ("sbuf", [128, 4 * OW], "bfloat16"),
+    "xr": ("sbuf", [128, 2 * OW], "bfloat16"),
+    "sm": ("sbuf", [128, 4 * 8], "float32"),
+    "tb": ("sbuf", [128, 4 * 128], "float32"),
+    "yb": ("sbuf", [128, 2 * 128], "bfloat16"),
     "ps0": ("psum", [128, 512], "float32"),
     "ps1": ("psum", [128, 512], "float32"),
     "ps2": ("psum", [128, 512], "float32"),
     "ps3": ("psum", [128, 512], "float32"),
     "pt0": ("psum", [128, 1024], "bfloat16"),
     "pt1": ("psum", [128, 1024], "bfloat16"),
-    "po0": ("psum", [128, 512], "float32"),
-    "po1": ("psum", [128, 512], "float32"),
+    "pt2": ("psum", [128, 1024], "bfloat16"),
+    "pt3": ("psum", [128, 1024], "bfloat16"),
 }
-SEMAPHORES = (["ldq", "qr", "snt", "st", "id0", "id1", "qx0", "qx1"]
-              + ["%s%d" % (n, i) for n in ("ld", "kv", "rs", "ch", "sS", "sM", "sE", "sT", "sC", "sL", "sO", "sV")
+SEMAPHORES = (["ldq", "qr", "snt", "st", "id0", "id1", "qx0", "qx1", "xa"]
+              + ["%s%d" % (n, i)
+                 for n in ("ld", "kv", "rs", "cb", "sS", "sM", "sE", "sT", "sC", "sL", "sO", "sV")
                  for i in range(4)])
 
 Exp = ActivationFunctionType.Exp
@@ -72,13 +73,16 @@ def _offs(s):
     return (KP, 0, 2 * KP) if s % 2 == 0 else (QP, QP + KP, 0)
 
 
+def _masks(topo, core, near, far):
+    m_off = topo.mask(core, far)
+    return m_off, _join([b for b in _bits(topo.mask(core, near)) if not (b & m_off)])
+
+
 def _rank(g, core, T, topo, cores, cls, work, p, s):
     S = T.sem
     ko, vo, qo = _offs(s)
     mine = work[p][s]
-    away = [work[p][h] for h in range(NH) if h != s]
-    m_off = topo.mask(core, away[0])
-    m_on = _join([b for b in _bits(topo.mask(core, mine)) if not (b & m_off)])
+    m_off, m_on = _masks(topo, core, mine, work[p][(s + 1) % NH])
     order = [(s + 1 + i) % NH for i in range(NH)]
     g.sync.dma_start(T.qs[:, :], T.q[:, :]).then_inc(S.ldq, 16)
     for n, h in enumerate(order):
@@ -100,47 +104,13 @@ def _rank(g, core, T, topo, cores, cls, work, p, s):
         g.remote_dma(T.land[:, PW * s:PW * s + PW], T.stage[:, PW * h:PW * h + PW], S["kv%d" % s], S.snt, pid, rid, m)
         sent += len(_bits(m))
     g.wait_ge(S.snt, sent)
-    tile = 2 * p + s // 2
     lo = 64 * (s % 2)
-    hi = lo + 64
-    V, A = g.vector, g.scalar
-    for i in range(NH):
-        h = (tile - i) % NH
-        ch, rs = S["ch%d" % h], S["rs%d" % h]
-        a0, b0 = (2 * h) * OS, (2 * h + 1) * OS
-        sm = 8 * h
-        ps = T["ps%d" % h]
-
-        def col(c):
-            return T.sm[lo:hi, sm + c:sm + c + 1]
-        V.wait_ge(rs, 8)
-        A.wait_ge(rs, 8)
-        V.tensor_tensor(col(0), T.res[lo:hi, a0 + 129:a0 + 130], T.res[lo:hi, b0 + 129:b0 + 130],
-                        AluOpType.min).then_inc(ch, 1)
-        A.wait_ge(ch, 1)
-        A.activation(col(1), T.res[lo:hi, a0 + 129:a0 + 130], Exp, bias=col(0), scale=-1.0).then_inc(ch, 1)
-        A.activation(col(2), T.res[lo:hi, b0 + 129:b0 + 130], Exp, bias=col(0), scale=-1.0).then_inc(ch, 1)
-        V.wait_ge(ch, 3)
-        V.tensor_scalar(col(3), T.res[lo:hi, a0 + 128:a0 + 129], col(1), None, AluOpType.mult).then_inc(ch, 1)
-        V.wait_ge(ch, 4)
-        V.tensor_scalar(col(4), T.res[lo:hi, b0 + 128:b0 + 129], col(2), col(3),
-                        AluOpType.mult, AluOpType.add).then_inc(ch, 1)
-        V.wait_ge(ch, 5)
-        V.reciprocal(col(5), col(4)).then_inc(ch, 1)
-        V.wait_ge(ch, 6)
-        V.tensor_scalar(T.sm[lo:hi, sm + 6:sm + 8], T.sm[lo:hi, sm + 1:sm + 3], col(5), None,
-                        AluOpType.mult).then_inc(ch, 1)
-        A.wait_ge(ch, 7)
-        V.wait_ge(ch, 7)
-        A.activation(ps[lo:hi, 0:128], T.res[lo:hi, a0:a0 + 128], Copy, scale=col(6)).then_inc(ch, 1)
-        V.tensor_scalar(T.tb[lo:hi, 128 * h:128 * h + 128], T.res[lo:hi, b0:b0 + 128], col(7), None,
-                        AluOpType.mult).then_inc(ch, 1)
-        V.wait_ge(ch, 9)
-        V.tensor_tensor(T.ysb[lo:hi, 128 * h:128 * h + 128], ps[lo:hi, 0:128], T.tb[lo:hi, 128 * h:128 * h + 128],
-                        AluOpType.add).then_inc(ch, 1)
-        g.sync.wait_ge(ch, 10)
-        g.sync.dma_start(T.y[:, 128 * h:128 * h + 128], T.ysb[lo:hi, 128 * h:128 * h + 128]).then_inc(S.st, 16)
-    g.sync.wait_ge(S.st, 16 * NH)
+    for h in range(NH):
+        n_fin = len(_bits(topo.mask(work[p][h], work[1 - p][h]))) // 4
+        qq = g.sync if h % 2 else g.scalar
+        qq.wait_ge(S["rs%d" % h], n_fin)
+        qq.dma_start(T.y[:, 128 * h:128 * h + 128], T.res[lo:lo + 64, 128 * h:128 * h + 128]).then_inc(S.st, 16)
+    g.wait_ge(S.st, 16 * NH)
 
 
 def _worker(g, core, T, topo, cores, cls, work, p, h):
@@ -151,9 +121,12 @@ def _worker(g, core, T, topo, cores, cls, work, p, h):
     g.affine_select(T.ident[:, :], T.ones[:, :], [[-1, 128]], AluOpType.is_equal, 0.0, 0, 1).then_inc(S.id1, 1)
     sent = 0
     far = [work[1 - p][hh] for hh in range(NH)]
-    eb = _bits(_join([0]) | topo.mask(core, far[0]))
+    eb = _bits(topo.mask(core, far[0]))
     per = len(eb) // NH
-    g.wait_ge(S.qr, len(_bits(topo.mask(cores[cls[p][h]], core))) - len(eb))
+    rk = cores[cls[p][h]]
+    r_off, r_on = _masks(topo, rk, core, work[p][(h + 1) % NH])
+    n_off, n_on = len(_bits(r_off)), len(_bits(r_on))
+    g.wait_ge(S.qr, n_on)
     trs = []
     for hh in range(NH):
         rid, pid, _ = topo.addr(far[hh])
@@ -163,10 +136,9 @@ def _worker(g, core, T, topo, cores, cls, work, p, h):
         sent += per
     g.remote_dma_fused(trs, local_sem=S.snt)
 
-    tiles = [(h + i) % 4 for i in range(4)]
+    tiles = [(1 - p, 0), (1 - p, 1), (p, 0), (p, 1)]
 
-    def qtile(t):
-        c, a = t // 2, t % 2
+    def qtile(c, a):
         if c == p:
             return T.land[:, 2 * PW * a + 2 * KP:2 * PW * a + 2 * KP + 2 * QP]
         return T.qx[:, 2 * QP * a:2 * QP * a + 2 * QP]
@@ -178,22 +150,22 @@ def _worker(g, core, T, topo, cores, cls, work, p, h):
     def vblk(j):
         o = PW * j + _offs(j)[1]
         return T.land[:, o:o + KP]
+
+    def cnt(j):
+        return n_on if j == h else n_off
     ps = [T["ps%d" % i] for i in range(4)]
-    pt = [T.pt0, T.pt1]
-    po = [T.po0, T.po1]
-    n_off = len(eb)
+    pt = [T["pt%d" % i] for i in range(4)]
     arr = [(h - 1 - i) % 4 for i in range(4)]
     events = [("k", arr[0]), ("x", 0), ("x", 1), ("k", arr[1]), ("k", arr[2]), ("k", arr[3])]
     havek, havex, done = [], [], []
     for kind, n in events:
         if kind == "k":
-            P.wait_ge(S["kv%d" % n], n_off)
+            P.wait_ge(S["kv%d" % n], cnt(n))
             havek.append(n)
         else:
             P.wait_ge(S["qx%d" % n], 2 * per)
             havex.append(n)
-        for i, t in enumerate(tiles):
-            c, a = t // 2, t % 2
+        for i, (c, a) in enumerate(tiles):
             ok = (2 * a in havek and 2 * a + 1 in havek) if c == p else (a in havex)
             if not ok:
                 continue
@@ -201,10 +173,10 @@ def _worker(g, core, T, topo, cores, cls, work, p, h):
                 if (i, j) in done:
                     continue
                 done.append((i, j))
-                P.matmul(ps[i][:, KP * j:KP * j + KP], qtile(t), kblk(j), True, True).then_inc(S["sS%d" % i], 1)
+                P.matmul(ps[i][:, KP * j:KP * j + KP], qtile(c, a), kblk(j), True, True).then_inc(S["sS%d" % i], 1)
 
     def nmcol(i):
-        return T.ob[:, OS * i + 129:OS * i + 130]
+        return T.ob[:, OW * i + 129:OW * i + 130]
 
     def v_max(i):
         V.wait_ge(S["sS%d" % i], 4)
@@ -217,53 +189,94 @@ def _worker(g, core, T, topo, cores, cls, work, p, h):
 
     def p_tr(i):
         P.wait_ge(S["sE%d" % i], 1)
-        if i >= 2:
-            P.wait_ge(S["sC%d" % (i - 2)], 1)
         for j in range(4):
-            P.transpose(pt[i % 2][:, 128 * j:128 * j + 128], T.pw[:, 512 * i + 128 * j:512 * i + 128 * j + 128],
+            P.transpose(pt[i][:, 128 * j:128 * j + 128], T.pw[:, 512 * i + 128 * j:512 * i + 128 * j + 128],
                         T.ident[:, :]).then_inc(S["sT%d" % i], 1)
 
     def v_cp(i):
         V.wait_ge(S["sT%d" % i], 4)
-        V.tensor_copy(T.pk[:, 512 * i:512 * i + 512], pt[i % 2][:, 0:512]).then_inc(S["sC%d" % i], 1)
-        V.tensor_copy(T.ob[:, OS * i + 128:OS * i + 129], T.lacc[:, i:i + 1]).then_inc(S["sL%d" % i], 1)
+        V.tensor_copy(T.pk[:, 512 * i:512 * i + 512], pt[i][:, 0:512]).then_inc(S["sC%d" % i], 1)
+        if i < 2:
+            V.tensor_copy(T.ob[:, OW * i + 128:OW * i + 129], T.lacc[:, i:i + 1]).then_inc(S["sL%d" % i], 1)
 
     def p_pv(i):
         P.wait_ge(S["sC%d" % i], 1)
-        if i >= 2:
-            P.wait_ge(S["sV%d" % (i - 2)], 1)
         for j in range(4):
-            P.matmul(po[i % 2][:, 0:128], T.pk[:, 512 * i + 128 * j:512 * i + 128 * j + 128], vblk(j),
+            P.matmul(ps[i][:, 0:128], T.pk[:, 512 * i + 128 * j:512 * i + 128 * j + 128], vblk(j),
                      j == 0, j == 3).then_inc(S["sO%d" % i], 1)
 
     def a_ev(i):
         A.wait_ge(S["sO%d" % i], 4)
-        A.activation(T.ob[:, OS * i:OS * i + 128], po[i % 2][:, 0:128], Copy).then_inc(S["sV%d" % i], 1)
+        A.activation(T.ob[:, OW * i:OW * i + 128], ps[i][:, 0:128], Copy).then_inc(S["sV%d" % i], 1)
 
-    for f, i in ((v_max, 0), (v_max, 1), (v_max, 2), (v_cp, 0), (v_max, 3), (v_cp, 1), (v_cp, 2), (v_cp, 3)):
+    def col(i, c):
+        return T.sm[:, 8 * i + c:8 * i + c + 1]
+
+    def xcol(i, c):
+        return T.xr[:, OW * (i - 2) + c:OW * (i - 2) + c + 1]
+
+    def v_j1(i):
+        V.wait_ge(S.xa, len(eb))
+        V.wait_ge(S["sM%d" % i], 1)
+        V.tensor_tensor(col(i, 0), nmcol(i), xcol(i, 129), AluOpType.min).then_inc(S["cb%d" % i], 1)
+
+    def a_j2(i):
+        A.wait_ge(S.xa, len(eb))
+        A.wait_ge(S["cb%d" % i], 1)
+        A.activation(col(i, 1), nmcol(i), Exp, bias=col(i, 0), scale=-1.0).then_inc(S["cb%d" % i], 1)
+        A.activation(col(i, 2), xcol(i, 129), Exp, bias=col(i, 0), scale=-1.0).then_inc(S["cb%d" % i], 1)
+
+    def v_j3(i):
+        cb = S["cb%d" % i]
+        V.wait_ge(cb, 3)
+        V.tensor_scalar(col(i, 3), T.lacc[:, i:i + 1], col(i, 1), None, AluOpType.mult).then_inc(cb, 1)
+        V.wait_ge(cb, 4)
+        V.tensor_scalar(col(i, 4), xcol(i, 128), col(i, 2), col(i, 3), AluOpType.mult, AluOpType.add).then_inc(cb, 1)
+        V.wait_ge(cb, 5)
+        V.reciprocal(col(i, 5), col(i, 4)).then_inc(cb, 1)
+        V.wait_ge(cb, 6)
+        V.tensor_scalar(T.sm[:, 8 * i + 6:8 * i + 8], T.sm[:, 8 * i + 1:8 * i + 3], col(i, 5), None,
+                        AluOpType.mult).then_inc(cb, 1)
+        V.wait_ge(cb, 7)
+        V.tensor_scalar(T.tb[:, 128 * i:128 * i + 128], T.xr[:, OW * (i - 2):OW * (i - 2) + 128], col(i, 7), None,
+                        AluOpType.mult).then_inc(cb, 1)
+
+    def a_j4(i):
+        A.wait_ge(S["cb%d" % i], 7)
+        A.wait_ge(S["sO%d" % i], 4)
+        A.activation(ps[i][:, 128:256], ps[i][:, 0:128], Copy, scale=col(i, 6)).then_inc(S["cb%d" % i], 1)
+
+    def v_j5(i):
+        V.wait_ge(S["cb%d" % i], 9)
+        V.tensor_tensor(T.yb[:, 128 * (i - 2):128 * (i - 2) + 128], ps[i][:, 128:256], T.tb[:, 128 * i:128 * i + 128],
+                        AluOpType.add).then_inc(S["cb%d" % i], 1)
+
+    for f, i in ((v_max, 0), (v_max, 1), (v_max, 2), (v_cp, 0), (v_max, 3), (v_cp, 1), (v_cp, 2), (v_cp, 3),
+                 (v_j1, 2), (v_j1, 3), (v_j3, 2), (v_j3, 3), (v_j5, 2), (v_j5, 3)):
         f(i)
-    for f, i in ((a_exp, 0), (a_exp, 1), (a_exp, 2), (a_ev, 0), (a_exp, 3), (a_ev, 1), (a_ev, 2), (a_ev, 3)):
+    for f, i in ((a_exp, 0), (a_exp, 1), (a_exp, 2), (a_ev, 0), (a_exp, 3), (a_ev, 1),
+                 (a_j2, 2), (a_j2, 3), (a_j4, 2), (a_j4, 3)):
         f(i)
     P.wait_ge(S.id1, 1)
     for f, i in ((p_tr, 0), (p_tr, 1), (p_pv, 0), (p_tr, 2), (p_pv, 1), (p_tr, 3), (p_pv, 2), (p_pv, 3)):
         f(i)
-    slot = (2 * h + p) * OS
-    for i, t in enumerate(tiles):
-        c, a = t // 2, t % 2
-        dsts = [cores[cls[c][2 * a]], cores[cls[c][2 * a + 1]]]
-        bs = _bits(topo.mask(core, dsts[0]) & topo.mask(core, dsts[1]) & _join(eb))
-        half = len(bs) // 2
+    for i in range(2):
         g.wait_ge(S["sV%d" % i], 1)
         g.wait_ge(S["sL%d" % i], 1)
-        trs = []
-        for n, d in enumerate(dsts):
-            rid, pid, _ = topo.addr(d)
-            trs.append(RemoteDMATransfer(dst_ids=[DstId(rid=rid, pnc=pid)],
-                                         dma_engine_mask=_join(bs[half * n:half * n + half]),
-                                         remote_sem=S["rs%d" % h], src=T.ob[:, OS * i:OS * i + OW],
-                                         dst=T.res[:, slot:slot + OW]))
-            sent += half
-        g.remote_dma_fused(trs, local_sem=S.snt)
+    rid, pid, _ = topo.addr(far[h])
+    g.remote_dma(T.xr[:, :], T.ob[:, 0:2 * OW], S.xa, S.snt, pid, rid, _join(eb))
+    sent += len(eb)
+    g.wait_ge(S.cb2, 10)
+    g.wait_ge(S.cb3, 10)
+    trs = []
+    for n in range(4):
+        rid, pid, _ = topo.addr(cores[cls[p][n]])
+        a = n // 2
+        trs.append(RemoteDMATransfer(dst_ids=[DstId(rid=rid, pnc=pid)], dma_engine_mask=_join(eb[per * n:per * n + per]),
+                                     remote_sem=S["rs%d" % h], src=T.yb[:, 128 * a:128 * a + 128],
+                                     dst=T.res[:, 128 * h:128 * h + 128]))
+        sent += per
+    g.remote_dma_fused(trs, local_sem=S.snt)
     g.wait_ge(S.snt, sent)
 
 

@@ -12,6 +12,7 @@ SCRATCH = {
     "qrel": ("sbuf", [128, NH * QP], "bfloat16"),
     "land": ("sbuf", [128, 4 * PW], "bfloat16"),
     "qx": ("sbuf", [128, 4 * QP], "bfloat16"),
+    "zz": ("sbuf", [128, 128], "bfloat16"),
     "ones": ("sbuf", [128, 128], "bfloat16"),
     "ident": ("sbuf", [128, 128], "bfloat16"),
     "pw": ("sbuf", [128, 4 * 512], "bfloat16"),
@@ -116,8 +117,10 @@ def _rank(g, core, T, topo, cores, cls, work, p, s):
 def _worker(g, core, T, topo, cores, cls, work, p, h):
     S = T.sem
     P, V, A = g.tensor, g.vector, g.scalar
-    V.memset(T.ones[:, :], 1.0).then_inc(S.id0, 1)
-    g.wait_ge(S.id0, 1)
+    V.memset(T.zz[:, :], 0.0).then_inc(S.id0, 1)
+    A.wait_ge(S.id0, 1)
+    A.activation(T.ones[:, :], T.zz[:, :], Exp).then_inc(S.id0, 1)
+    g.wait_ge(S.id0, 2)
     g.affine_select(T.ident[:, :], T.ones[:, :], [[-1, 128]], AluOpType.is_equal, 0.0, 0, 1).then_inc(S.id1, 1)
     sent = 0
     far = [work[1 - p][hh] for hh in range(NH)]
@@ -254,11 +257,11 @@ def _worker(g, core, T, topo, cores, cls, work, p, h):
     for f, i in ((v_max, 0), (v_max, 1), (v_max, 2), (v_cp, 0), (v_max, 3), (v_cp, 1), (v_cp, 2), (v_cp, 3),
                  (v_j1, 2), (v_j1, 3), (v_j3, 2), (v_j3, 3), (v_j5, 2), (v_j5, 3)):
         f(i)
-    for f, i in ((a_exp, 0), (a_exp, 1), (a_exp, 2), (a_ev, 0), (a_exp, 3), (a_ev, 1),
+    for f, i in ((a_exp, 0), (a_exp, 1), (a_exp, 2), (a_exp, 3), (a_ev, 0), (a_ev, 1),
                  (a_j2, 2), (a_j2, 3), (a_j4, 2), (a_j4, 3)):
         f(i)
     P.wait_ge(S.id1, 1)
-    for f, i in ((p_tr, 0), (p_tr, 1), (p_pv, 0), (p_tr, 2), (p_pv, 1), (p_tr, 3), (p_pv, 2), (p_pv, 3)):
+    for f, i in ((p_tr, 0), (p_tr, 1), (p_pv, 0), (p_pv, 1), (p_tr, 2), (p_tr, 3), (p_pv, 2), (p_pv, 3)):
         f(i)
     for i in range(2):
         g.wait_ge(S["sV%d" % i], 1)

@@ -20,8 +20,8 @@ SCRATCH = {
     "lacc": ("sbuf", [128, 4], "float32"),
     "ob": ("sbuf", [128, 4 * OW], "bfloat16"),
     "xr": ("sbuf", [128, 2 * OW], "bfloat16"),
-    "sm": ("sbuf", [128, 4 * 8], "float32"),
-    "tb": ("sbuf", [128, 4 * 128], "float32"),
+    "sm": ("sbuf", [128, 8], "float32"),
+    "dg": ("sbuf", [128, 2 * 128], "bfloat16"),
     "yb": ("sbuf", [128, 2 * 128], "bfloat16"),
     "ps0": ("psum", [128, 512], "float32"),
     "ps1": ("psum", [128, 512], "float32"),
@@ -32,9 +32,9 @@ SCRATCH = {
     "pt2": ("psum", [128, 1024], "bfloat16"),
     "pt3": ("psum", [128, 1024], "bfloat16"),
 }
-SEMAPHORES = (["ldq", "qr", "snt", "st", "id0", "id1", "qx0", "qx1", "xa"]
+SEMAPHORES = (["ldq", "qr", "snt", "st", "id0", "id1", "qx0", "qx1", "xa", "jn"]
               + ["%s%d" % (n, i)
-                 for n in ("ld", "kv", "rs", "cb", "sS", "sM", "sE", "sT", "sC", "sL", "sO", "sV")
+                 for n in ("ld", "kv", "rs", "sS", "sM", "sE", "sT", "sC", "sL", "sO", "sV")
                  for i in range(4)])
 
 Exp = ActivationFunctionType.Exp
@@ -159,24 +159,32 @@ def _worker(g, core, T, topo, cores, cls, work, p, h):
     ps = [T["ps%d" % i] for i in range(4)]
     pt = [T["pt%d" % i] for i in range(4)]
     arr = [(h - 1 - i) % 4 for i in range(4)]
-    events = [("k", arr[0]), ("x", 0), ("x", 1), ("k", arr[1]), ("k", arr[2]), ("k", arr[3])]
-    havek, havex, done = [], [], []
-    for kind, n in events:
-        if kind == "k":
-            P.wait_ge(S["kv%d" % n], cnt(n))
-            havek.append(n)
-        else:
-            P.wait_ge(S["qx%d" % n], 2 * per)
-            havex.append(n)
-        for i, (c, a) in enumerate(tiles):
-            ok = (2 * a in havek and 2 * a + 1 in havek) if c == p else (a in havex)
-            if not ok:
-                continue
-            for j in havek:
-                if (i, j) in done:
-                    continue
+    done = []
+
+    def p_sc(i, js):
+        c, a = tiles[i]
+        for j in js:
+            if (i, j) not in done:
                 done.append((i, j))
                 P.matmul(ps[i][:, KP * j:KP * j + KP], qtile(c, a), kblk(j), True, True).then_inc(S["sS%d" % i], 1)
+
+    havek = []
+    for n in arr[0:3]:
+        P.wait_ge(S["kv%d" % n], cnt(n))
+        havek.append(n)
+        for i in (2, 3):
+            a = tiles[i][1]
+            if 2 * a in havek and 2 * a + 1 in havek:
+                p_sc(i, havek)
+    P.wait_ge(S.qx0, 2 * per)
+    p_sc(0, havek)
+    P.wait_ge(S["kv%d" % arr[3]], cnt(arr[3]))
+    havek.append(arr[3])
+    p_sc(0, havek)
+    P.wait_ge(S.qx1, 2 * per)
+    p_sc(1, havek)
+    p_sc(2, havek)
+    p_sc(3, havek)
 
     def nmcol(i):
         return T.ob[:, OW * i + 129:OW * i + 130]
@@ -206,71 +214,72 @@ def _worker(g, core, T, topo, cores, cls, work, p, h):
         P.wait_ge(S["sC%d" % i], 1)
         for j in range(4):
             P.matmul(ps[i][:, 0:128], T.pk[:, 512 * i + 128 * j:512 * i + 128 * j + 128], vblk(j),
-                     j == 0, j == 3).then_inc(S["sO%d" % i], 1)
+                     j == 0, j == 3 and i < 2).then_inc(S["sO%d" % i], 1)
 
     def a_ev(i):
         A.wait_ge(S["sO%d" % i], 4)
         A.activation(T.ob[:, OW * i:OW * i + 128], ps[i][:, 0:128], Copy).then_inc(S["sV%d" % i], 1)
 
-    def col(i, c):
-        return T.sm[:, 8 * i + c:8 * i + c + 1]
+    jn = S.jn
 
     def xcol(i, c):
         return T.xr[:, OW * (i - 2) + c:OW * (i - 2) + c + 1]
 
-    def v_j1(i):
-        V.wait_ge(S.xa, len(eb))
+    def v_jd(i):
         V.wait_ge(S["sM%d" % i], 1)
-        V.tensor_tensor(col(i, 0), nmcol(i), xcol(i, 129), AluOpType.min).then_inc(S["cb%d" % i], 1)
+        V.tensor_scalar(T.sm[:, i - 2:i - 1], nmcol(i), xcol(i, 129), 30.0, AluOpType.subtract,
+                        AluOpType.min).then_inc(jn, 1)
 
-    def a_j2(i):
-        A.wait_ge(S.xa, len(eb))
-        A.wait_ge(S["cb%d" % i], 1)
-        A.activation(col(i, 1), nmcol(i), Exp, bias=col(i, 0), scale=-1.0).then_inc(S["cb%d" % i], 1)
-        A.activation(col(i, 2), xcol(i, 129), Exp, bias=col(i, 0), scale=-1.0).then_inc(S["cb%d" % i], 1)
+    def v_jg(i):
+        V.tensor_scalar(T.dg[:, 128 * (i - 2):128 * (i - 2) + 128], T.ident[:, :], T.sm[:, i:i + 1], None,
+                        AluOpType.mult).then_inc(S["sL%d" % i], 1)
 
-    def v_j3(i):
-        cb = S["cb%d" % i]
-        V.wait_ge(cb, 3)
-        V.tensor_scalar(col(i, 3), T.lacc[:, i:i + 1], col(i, 1), None, AluOpType.mult).then_inc(cb, 1)
-        V.wait_ge(cb, 4)
-        V.tensor_scalar(col(i, 4), xcol(i, 128), col(i, 2), col(i, 3), AluOpType.mult, AluOpType.add).then_inc(cb, 1)
-        V.wait_ge(cb, 5)
-        V.reciprocal(col(i, 5), col(i, 4)).then_inc(cb, 1)
-        V.wait_ge(cb, 6)
-        V.tensor_scalar(T.sm[:, 8 * i + 6:8 * i + 8], T.sm[:, 8 * i + 1:8 * i + 3], col(i, 5), None,
-                        AluOpType.mult).then_inc(cb, 1)
-        V.wait_ge(cb, 7)
-        V.tensor_scalar(T.tb[:, 128 * i:128 * i + 128], T.xr[:, OW * (i - 2):OW * (i - 2) + 128], col(i, 7), None,
-                        AluOpType.mult).then_inc(cb, 1)
+    def v_jl(i):
+        V.tensor_scalar(T.sm[:, i + 2:i + 3], xcol(i, 128), T.sm[:, i:i + 1], T.lacc[:, i:i + 1], AluOpType.mult,
+                        AluOpType.add).then_inc(jn, 1)
 
-    def a_j4(i):
-        A.wait_ge(S["cb%d" % i], 7)
-        A.wait_ge(S["sO%d" % i], 4)
-        A.activation(ps[i][:, 128:256], ps[i][:, 0:128], Copy, scale=col(i, 6)).then_inc(S["cb%d" % i], 1)
+    def p_jm(i):
+        P.wait_ge(S["sL%d" % i], 1)
+        P.matmul(ps[i][:, 0:128], T.dg[:, 128 * (i - 2):128 * (i - 2) + 128], T.xr[:, OW * (i - 2):OW * (i - 2) + 128],
+                 False, True).then_inc(S["sO%d" % i], 1)
 
-    def v_j5(i):
-        V.wait_ge(S["cb%d" % i], 9)
-        V.tensor_tensor(T.yb[:, 128 * (i - 2):128 * (i - 2) + 128], ps[i][:, 128:256], T.tb[:, 128 * i:128 * i + 128],
-                        AluOpType.add).then_inc(S["cb%d" % i], 1)
+    def a_jy(i):
+        A.wait_ge(S["sO%d" % i], 5)
+        A.activation(T.yb[:, 128 * (i - 2):128 * (i - 2) + 128], ps[i][:, 0:128], Copy,
+                     scale=T.sm[:, i + 4:i + 5]).then_inc(S["sV%d" % i], 1)
 
-    for f, i in ((v_max, 0), (v_max, 1), (v_max, 2), (v_cp, 0), (v_max, 3), (v_cp, 1), (v_cp, 2), (v_cp, 3),
-                 (v_j1, 2), (v_j1, 3), (v_j3, 2), (v_j3, 3), (v_j5, 2), (v_j5, 3)):
+    for f, i in ((v_max, 0), (v_max, 1), (v_max, 2), (v_cp, 0), (v_cp, 1), (v_max, 3), (v_cp, 2), (v_cp, 3)):
         f(i)
-    for f, i in ((a_exp, 0), (a_exp, 1), (a_exp, 2), (a_exp, 3), (a_ev, 0), (a_ev, 1),
-                 (a_j2, 2), (a_j2, 3), (a_j4, 2), (a_j4, 3)):
+    V.wait_ge(S.id1, 1)
+    V.wait_ge(S.xa, len(eb))
+    v_jd(2)
+    v_jd(3)
+    V.wait_ge(jn, 3)
+    for f, i in ((v_jg, 2), (v_jg, 3), (v_jl, 2), (v_jl, 3)):
         f(i)
+    V.wait_ge(jn, 5)
+    V.reciprocal(T.sm[:, 6:8], T.sm[:, 4:6]).then_inc(jn, 1)
+    for f, i in ((a_exp, 0), (a_exp, 1), (a_exp, 2), (a_ev, 0), (a_ev, 1), (a_exp, 3)):
+        f(i)
+    A.wait_ge(jn, 2)
+    A.activation(T.sm[:, 2:4], T.sm[:, 0:2], Exp).then_inc(jn, 1)
+    A.wait_ge(jn, 6)
+    a_jy(2)
+    a_jy(3)
     P.wait_ge(S.id1, 1)
     for f, i in ((p_tr, 0), (p_tr, 1), (p_pv, 0), (p_pv, 1), (p_tr, 2), (p_tr, 3), (p_pv, 2), (p_pv, 3)):
         f(i)
+    P.wait_ge(S.xa, len(eb))
+    p_jm(2)
+    p_jm(3)
     for i in range(2):
         g.wait_ge(S["sV%d" % i], 1)
         g.wait_ge(S["sL%d" % i], 1)
     rid, pid, _ = topo.addr(far[h])
     g.remote_dma(T.xr[:, :], T.ob[:, 0:2 * OW], S.xa, S.snt, pid, rid, _join(eb))
     sent += len(eb)
-    g.wait_ge(S.cb2, 10)
-    g.wait_ge(S.cb3, 10)
+    g.wait_ge(S.sV2, 1)
+    g.wait_ge(S.sV3, 1)
     trs = []
     for n in range(4):
         rid, pid, _ = topo.addr(cores[cls[p][n]])

@@ -3,7 +3,6 @@ from concourse.mybir import AluOpType, AxisListType, ActivationFunctionType
 
 NH, QP, KP = 4, 64, 128
 PW = KP + KP + QP
-OW = 130
 
 SCRATCH = {
     "qs": ("sbuf", [128, NH * QP], "bfloat16"),
@@ -18,8 +17,11 @@ SCRATCH = {
     "pw": ("sbuf", [128, 4 * 512], "bfloat16"),
     "pk": ("sbuf", [128, 4 * 512], "bfloat16"),
     "lacc": ("sbuf", [128, 4], "float32"),
-    "ob": ("sbuf", [128, 4 * OW], "bfloat16"),
-    "xr": ("sbuf", [128, 2 * OW], "bfloat16"),
+    "ob": ("sbuf", [128, 2 * 128], "bfloat16"),
+    "xr": ("sbuf", [128, 2 * 128], "bfloat16"),
+    "st": ("sbuf", [128, 4], "bfloat16"),
+    "xs": ("sbuf", [128, 4], "bfloat16"),
+    "nmo": ("sbuf", [128, 2], "bfloat16"),
     "sm": ("sbuf", [128, 8], "float32"),
     "dg": ("sbuf", [128, 2 * 128], "bfloat16"),
     "yb": ("sbuf", [128, 2 * 128], "bfloat16"),
@@ -32,7 +34,7 @@ SCRATCH = {
     "pt2": ("psum", [128, 1024], "bfloat16"),
     "pt3": ("psum", [128, 1024], "bfloat16"),
 }
-SEMAPHORES = (["ldq", "qr", "snt", "st", "id0", "id1", "qx0", "qx1", "xa", "jn"]
+SEMAPHORES = (["ldq", "qr", "snt", "st", "id0", "id1", "qx0", "qx1", "xa2", "xa3", "xsa", "jn", "lc"]
               + ["%s%d" % (n, i)
                  for n in ("ld", "kv", "rs", "sS", "sM", "sE", "sT", "sC", "sL", "sO", "sV")
                  for i in range(4)])
@@ -107,7 +109,7 @@ def _rank(g, core, T, topo, cores, cls, work, p, s):
     g.wait_ge(S.snt, sent)
     lo = 64 * (s % 2)
     for h in range(NH):
-        n_fin = len(_bits(topo.mask(work[p][h], work[1 - p][h]))) // 4
+        n_fin = len(_bits(topo.mask(work[p][h], work[1 - p][h]))) // 2
         qq = g.sync if h % 2 else g.scalar
         qq.wait_ge(S["rs%d" % h], n_fin)
         qq.dma_start(T.y[:, 128 * h:128 * h + 128], T.res[lo:lo + 64, 128 * h:128 * h + 128]).then_inc(S.st, 16)
@@ -187,7 +189,7 @@ def _worker(g, core, T, topo, cores, cls, work, p, h):
     p_sc(3, havek)
 
     def nmcol(i):
-        return T.ob[:, OW * i + 129:OW * i + 130]
+        return T.st[:, 2 + i:3 + i] if i < 2 else T.nmo[:, i - 2:i - 1]
 
     def v_max(i):
         V.wait_ge(S["sS%d" % i], 4)
@@ -207,8 +209,11 @@ def _worker(g, core, T, topo, cores, cls, work, p, h):
     def v_cp(i):
         V.wait_ge(S["sT%d" % i], 4)
         V.tensor_copy(T.pk[:, 512 * i:512 * i + 512], pt[i][:, 0:512]).then_inc(S["sC%d" % i], 1)
-        if i < 2:
-            V.tensor_copy(T.ob[:, OW * i + 128:OW * i + 129], T.lacc[:, i:i + 1]).then_inc(S["sL%d" % i], 1)
+
+    def v_lc(i):
+        V.wait_ge(S.sE0, 1)
+        V.wait_ge(S.sE1, 1)
+        V.tensor_copy(T.st[:, 0:2], T.lacc[:, 0:2]).then_inc(S.lc, 1)
 
     def p_pv(i):
         P.wait_ge(S["sC%d" % i], 1)
@@ -218,16 +223,13 @@ def _worker(g, core, T, topo, cores, cls, work, p, h):
 
     def a_ev(i):
         A.wait_ge(S["sO%d" % i], 4)
-        A.activation(T.ob[:, OW * i:OW * i + 128], ps[i][:, 0:128], Copy).then_inc(S["sV%d" % i], 1)
+        A.activation(T.ob[:, 128 * i:128 * i + 128], ps[i][:, 0:128], Copy).then_inc(S["sV%d" % i], 1)
 
     jn = S.jn
 
-    def xcol(i, c):
-        return T.xr[:, OW * (i - 2) + c:OW * (i - 2) + c + 1]
-
     def v_jd(i):
         V.wait_ge(S["sM%d" % i], 1)
-        V.tensor_scalar(T.sm[:, i - 2:i - 1], nmcol(i), xcol(i, 129), 30.0, AluOpType.subtract,
+        V.tensor_scalar(T.sm[:, i - 2:i - 1], nmcol(i), T.xs[:, i:i + 1], 30.0, AluOpType.subtract,
                         AluOpType.min).then_inc(jn, 1)
 
     def v_jg(i):
@@ -235,60 +237,63 @@ def _worker(g, core, T, topo, cores, cls, work, p, h):
                         AluOpType.mult).then_inc(S["sL%d" % i], 1)
 
     def v_jl(i):
-        V.tensor_scalar(T.sm[:, i + 2:i + 3], xcol(i, 128), T.sm[:, i:i + 1], T.lacc[:, i:i + 1], AluOpType.mult,
+        V.tensor_scalar(T.sm[:, i + 2:i + 3], T.xs[:, i - 2:i - 1], T.sm[:, i:i + 1], T.lacc[:, i:i + 1], AluOpType.mult,
                         AluOpType.add).then_inc(jn, 1)
 
     def p_jm(i):
+        P.wait_ge(S["xa%d" % i], len(eb))
         P.wait_ge(S["sL%d" % i], 1)
-        P.matmul(ps[i][:, 0:128], T.dg[:, 128 * (i - 2):128 * (i - 2) + 128], T.xr[:, OW * (i - 2):OW * (i - 2) + 128],
+        P.matmul(ps[i][:, 0:128], T.dg[:, 128 * (i - 2):128 * (i - 2) + 128], T.xr[:, 128 * (i - 2):128 * (i - 2) + 128],
                  False, True).then_inc(S["sO%d" % i], 1)
 
-    def a_jy(i):
-        A.wait_ge(S["sO%d" % i], 5)
-        A.activation(T.yb[:, 128 * (i - 2):128 * (i - 2) + 128], ps[i][:, 0:128], Copy,
-                     scale=T.sm[:, i + 4:i + 5]).then_inc(S["sV%d" % i], 1)
-
-    for f, i in ((v_max, 0), (v_max, 1), (v_max, 2), (v_cp, 0), (v_cp, 1), (v_max, 3), (v_cp, 2), (v_cp, 3)):
+    for f, i in ((v_max, 0), (v_max, 1), (v_max, 2), (v_cp, 0), (v_lc, 0), (v_cp, 1), (v_max, 3), (v_cp, 2)):
         f(i)
     V.wait_ge(S.id1, 1)
-    V.wait_ge(S.xa, len(eb))
+    V.wait_ge(S.xsa, len(eb))
     v_jd(2)
     v_jd(3)
     V.wait_ge(jn, 3)
-    for f, i in ((v_jg, 2), (v_jg, 3), (v_jl, 2), (v_jl, 3)):
+    for f, i in ((v_jg, 2), (v_jg, 3), (v_cp, 3), (v_jl, 2), (v_jl, 3)):
         f(i)
     V.wait_ge(jn, 5)
     V.reciprocal(T.sm[:, 6:8], T.sm[:, 4:6]).then_inc(jn, 1)
+    V.wait_ge(jn, 6)
+    V.wait_ge(S.sO3, 5)
+    V.tensor_scalar(T.yb[:, 128:256], ps[3][:, 0:128], T.sm[:, 7:8], None, AluOpType.mult).then_inc(S.sV3, 1)
     for f, i in ((a_exp, 0), (a_exp, 1), (a_exp, 2), (a_ev, 0), (a_ev, 1), (a_exp, 3)):
         f(i)
     A.wait_ge(jn, 2)
     A.activation(T.sm[:, 2:4], T.sm[:, 0:2], Exp).then_inc(jn, 1)
     A.wait_ge(jn, 6)
-    a_jy(2)
-    a_jy(3)
+    A.wait_ge(S.sO2, 5)
+    A.activation(T.yb[:, 0:128], ps[2][:, 0:128], Copy, scale=T.sm[:, 6:7]).then_inc(S.sV2, 1)
     P.wait_ge(S.id1, 1)
-    for f, i in ((p_tr, 0), (p_tr, 1), (p_pv, 0), (p_pv, 1), (p_tr, 2), (p_tr, 3), (p_pv, 2), (p_pv, 3)):
+    for f, i in ((p_tr, 0), (p_tr, 1), (p_pv, 0), (p_pv, 1), (p_tr, 2), (p_tr, 3), (p_pv, 2), (p_jm, 2), (p_pv, 3),
+                 (p_jm, 3)):
         f(i)
-    P.wait_ge(S.xa, len(eb))
-    p_jm(2)
-    p_jm(3)
+    rid, pid, _ = topo.addr(far[h])
+    g.wait_ge(S.sM0, 1)
+    g.wait_ge(S.sM1, 1)
+    g.wait_ge(S.lc, 1)
+    g.remote_dma(T.xs[:, :], T.st[:, :], S.xsa, S.snt, pid, rid, _join(eb))
+    sent += len(eb)
     for i in range(2):
         g.wait_ge(S["sV%d" % i], 1)
-        g.wait_ge(S["sL%d" % i], 1)
-    rid, pid, _ = topo.addr(far[h])
-    g.remote_dma(T.xr[:, :], T.ob[:, 0:2 * OW], S.xa, S.snt, pid, rid, _join(eb))
-    sent += len(eb)
-    g.wait_ge(S.sV2, 1)
-    g.wait_ge(S.sV3, 1)
-    trs = []
-    for n in range(4):
-        rid, pid, _ = topo.addr(cores[cls[p][n]])
-        a = n // 2
-        trs.append(RemoteDMATransfer(dst_ids=[DstId(rid=rid, pnc=pid)], dma_engine_mask=_join(eb[per * n:per * n + per]),
-                                     remote_sem=S["rs%d" % h], src=T.yb[:, 128 * a:128 * a + 128],
-                                     dst=T.res[:, 128 * h:128 * h + 128]))
-        sent += per
-    g.remote_dma_fused(trs, local_sem=S.snt)
+        g.remote_dma(T.xr[:, 128 * i:128 * i + 128], T.ob[:, 128 * i:128 * i + 128], S["xa%d" % (i + 2)], S.snt, pid, rid,
+                     _join(eb))
+        sent += len(eb)
+    half = len(eb) // 2
+    for a in range(2):
+        g.wait_ge(S["sV%d" % (a + 2)], 1)
+        trs = []
+        for b in range(2):
+            rid, pid, _ = topo.addr(cores[cls[p][2 * a + b]])
+            trs.append(RemoteDMATransfer(dst_ids=[DstId(rid=rid, pnc=pid)],
+                                         dma_engine_mask=_join(eb[half * b:half * b + half]),
+                                         remote_sem=S["rs%d" % h], src=T.yb[:, 128 * a:128 * a + 128],
+                                         dst=T.res[:, 128 * h:128 * h + 128]))
+            sent += half
+        g.remote_dma_fused(trs, local_sem=S.snt)
     g.wait_ge(S.snt, sent)
 
 

from concourse.bass import DstId, RemoteDMATransfer
from concourse.mybir import AluOpType, AxisListType, ActivationFunctionType

NH, QP, KP = 4, 64, 128
PW = KP + KP + QP

SCRATCH = {
    "qs": ("sbuf", [128, NH * QP], "bfloat16"),
    "stage": ("sbuf", [128, NH * PW], "bfloat16"),
    "res": ("sbuf", [128, NH * 128], "bfloat16"),
    "qrel": ("sbuf", [128, NH * QP], "bfloat16"),
    "land": ("sbuf", [128, 4 * PW], "bfloat16"),
    "qx": ("sbuf", [128, 4 * QP], "bfloat16"),
    "zz": ("sbuf", [128, 128], "bfloat16"),
    "ones": ("sbuf", [128, 128], "bfloat16"),
    "ident": ("sbuf", [128, 128], "bfloat16"),
    "pw": ("sbuf", [128, 4 * 512], "bfloat16"),
    "pk": ("sbuf", [128, 4 * 512], "bfloat16"),
    "lacc": ("sbuf", [128, 4], "float32"),
    "ob": ("sbuf", [128, 2 * 128], "bfloat16"),
    "xr": ("sbuf", [128, 2 * 128], "bfloat16"),
    "st": ("sbuf", [128, 4], "bfloat16"),
    "xs": ("sbuf", [128, 4], "bfloat16"),
    "nmo": ("sbuf", [128, 2], "bfloat16"),
    "sm": ("sbuf", [128, 8], "float32"),
    "dg": ("sbuf", [128, 2 * 128], "bfloat16"),
    "yb": ("sbuf", [128, 2 * 128], "bfloat16"),
    "ps0": ("psum", [128, 512], "float32"),
    "ps1": ("psum", [128, 512], "float32"),
    "ps2": ("psum", [128, 512], "float32"),
    "ps3": ("psum", [128, 512], "float32"),
    "pt0": ("psum", [128, 1024], "bfloat16"),
    "pt1": ("psum", [128, 1024], "bfloat16"),
    "pt2": ("psum", [128, 1024], "bfloat16"),
    "pt3": ("psum", [128, 1024], "bfloat16"),
}
SEMAPHORES = (["ldq", "qr", "snt", "st", "id0", "id1", "qx0", "qx1", "xa2", "xa3", "xsa", "jn", "lc"]
              + ["%s%d" % (n, i)
                 for n in ("ld", "kv", "rs", "sS", "sM", "sE", "sT", "sC", "sL", "sO", "sV")
                 for i in range(4)])

Exp = ActivationFunctionType.Exp
Copy = ActivationFunctionType.Copy


def _bits(m):
    return [1 << e for e in range(m.bit_length()) if (m >> e) & 1]


def _join(bs):
    m = 0
    for b in bs:
        m |= b
    return m


def _plan(T, topo):
    cores = list(T.cores)
    c0 = topo.chip(cores[0])
    cls = [[], []]
    for r, c in enumerate(cores):
        ch = topo.chip(c)
        cls[0 if (ch == c0 or topo.same_plane(ch, c0)) else 1].append(r)
    work = [[None] * NH, [None] * NH]
    for p in range(2):
        for h in range(NH):
            rc = cores[cls[p][h]]
            cand = [c for c in range(topo.CHIPS * topo.CORES_PER_CHIP)
                    if topo.chip(c) == topo.chip(rc) and c not in cores and topo.die(c) == topo.die(rc)
                    and all(topo.may_write(c, d) for d in cores)]
            work[p][h] = cand[0]
    return cores, cls, work


def _offs(s):
    return (KP, 0, 2 * KP) if s % 2 == 0 else (QP, QP + KP, 0)


def _masks(topo, core, near, far):
    m_off = topo.mask(core, far)
    return m_off, _join([b for b in _bits(topo.mask(core, near)) if not (b & m_off)])


def _rank(g, core, T, topo, cores, cls, work, p, s):
    S = T.sem
    ko, vo, qo = _offs(s)
    mine = work[p][s]
    m_off, m_on = _masks(topo, core, mine, work[p][(s + 1) % NH])
    order = [(s + 1 + i) % NH for i in range(NH)]
    g.sync.dma_start(T.qs[:, :], T.q[:, :]).then_inc(S.ldq, 16)
    for n, h in enumerate(order):
        b = PW * h
        g.sync.dma_start(T.stage[:, b + ko:b + ko + KP], T.k[:, KP * h:KP * h + KP]).then_inc(S["ld%d" % h], 16)
        g.scalar.dma_start(T.stage[:, b + vo:b + vo + KP], T.v[:, KP * h:KP * h + KP]).then_inc(S["ld%d" % h], 16)
        qq = g.sync if n % 2 else g.scalar
        qq.dma_start(T.stage[:, b + qo:b + qo + QP], T.q[:, QP * h:QP * h + QP]).then_inc(S["ld%d" % h], 16)
    sent = 0
    rid, pid, _ = topo.addr(mine)
    g.wait_ge(S.ldq, 16)
    g.remote_dma(T.qrel[:, :], T.qs[:, :], S.qr, S.snt, pid, rid, m_on)
    sent += len(_bits(m_on))
    for h in order:
        dst = work[p][h]
        m = m_on if dst == mine else m_off
        rid, pid, _ = topo.addr(dst)
        g.wait_ge(S["ld%d" % h], 48)
        g.remote_dma(T.land[:, PW * s:PW * s + PW], T.stage[:, PW * h:PW * h + PW], S["kv%d" % s], S.snt, pid, rid, m)
        sent += len(_bits(m))
    g.wait_ge(S.snt, sent)
    lo = 64 * (s % 2)
    for h in range(NH):
        n_fin = len(_bits(topo.mask(work[p][h], work[1 - p][h]))) // 2
        qq = g.sync if h % 2 else g.scalar
        qq.wait_ge(S["rs%d" % h], n_fin)
        qq.dma_start(T.y[:, 128 * h:128 * h + 128], T.res[lo:lo + 64, 128 * h:128 * h + 128]).then_inc(S.st, 16)
    g.wait_ge(S.st, 16 * NH)


def _worker(g, core, T, topo, cores, cls, work, p, h):
    S = T.sem
    P, V, A = g.tensor, g.vector, g.scalar
    V.memset(T.zz[:, :], 0.0).then_inc(S.id0, 1)
    A.wait_ge(S.id0, 1)
    A.activation(T.ones[:, :], T.zz[:, :], Exp).then_inc(S.id0, 1)
    g.wait_ge(S.id0, 2)
    g.affine_select(T.ident[:, :], T.ones[:, :], [[-1, 128]], AluOpType.is_equal, 0.0, 0, 1).then_inc(S.id1, 1)
    sent = 0
    far = [work[1 - p][hh] for hh in range(NH)]
    eb = _bits(topo.mask(core, far[0]))
    per = len(eb) // NH
    rk = cores[cls[p][h]]
    r_off, r_on = _masks(topo, rk, core, work[p][(h + 1) % NH])
    n_off, n_on = len(_bits(r_off)), len(_bits(r_on))
    g.wait_ge(S.qr, n_on)
    trs = []
    for hh in range(NH):
        rid, pid, _ = topo.addr(far[hh])
        trs.append(RemoteDMATransfer(dst_ids=[DstId(rid=rid, pnc=pid)], dma_engine_mask=_join(eb[per * hh:per * hh + per]),
                                     remote_sem=S["qx%d" % (h // 2)], src=T.qrel[:, QP * hh:QP * hh + QP],
                                     dst=T.qx[:, QP * h:QP * h + QP]))
        sent += per
    g.remote_dma_fused(trs, local_sem=S.snt)

    tiles = [(1 - p, 0), (1 - p, 1), (p, 0), (p, 1)]

    def qtile(c, a):
        if c == p:
            return T.land[:, 2 * PW * a + 2 * KP:2 * PW * a + 2 * KP + 2 * QP]
        return T.qx[:, 2 * QP * a:2 * QP * a + 2 * QP]

    def kblk(j):
        o = PW * j + _offs(j)[0]
        return T.land[:, o:o + KP]

    def vblk(j):
        o = PW * j + _offs(j)[1]
        return T.land[:, o:o + KP]

    def cnt(j):
        return n_on if j == h else n_off
    ps = [T["ps%d" % i] for i in range(4)]
    pt = [T["pt%d" % i] for i in range(4)]
    arr = [(h - 1 - i) % 4 for i in range(4)]
    done = []

    def p_sc(i, js):
        c, a = tiles[i]
        for j in js:
            if (i, j) not in done:
                done.append((i, j))
                P.matmul(ps[i][:, KP * j:KP * j + KP], qtile(c, a), kblk(j), True, True).then_inc(S["sS%d" % i], 1)

    havek = []
    for n in arr[0:3]:
        P.wait_ge(S["kv%d" % n], cnt(n))
        havek.append(n)
        for i in (2, 3):
            a = tiles[i][1]
            if 2 * a in havek and 2 * a + 1 in havek:
                p_sc(i, havek)
    P.wait_ge(S.qx0, 2 * per)
    p_sc(0, havek)
    P.wait_ge(S["kv%d" % arr[3]], cnt(arr[3]))
    havek.append(arr[3])
    p_sc(0, havek)
    P.wait_ge(S.qx1, 2 * per)
    p_sc(1, havek)
    p_sc(2, havek)
    p_sc(3, havek)

    def nmcol(i):
        return T.st[:, 2 + i:3 + i] if i < 2 else T.nmo[:, i - 2:i - 1]

    def v_max(i):
        V.wait_ge(S["sS%d" % i], 4)
        V.tensor_reduce(nmcol(i), ps[i][:, :], AxisListType.X, AluOpType.max, negate=True).then_inc(S["sM%d" % i], 1)

    def a_exp(i):
        A.wait_ge(S["sM%d" % i], 1)
        A.activation(T.pw[:, 512 * i:512 * i + 512], ps[i][:, :], Exp, bias=nmcol(i),
                     accum_out=T.lacc[:, i:i + 1]).then_inc(S["sE%d" % i], 1)

    def p_tr(i):
        P.wait_ge(S["sE%d" % i], 1)
        for j in range(4):
            P.transpose(pt[i][:, 128 * j:128 * j + 128], T.pw[:, 512 * i + 128 * j:512 * i + 128 * j + 128],
                        T.ident[:, :]).then_inc(S["sT%d" % i], 1)

    def v_cp(i):
        V.wait_ge(S["sT%d" % i], 4)
        V.tensor_copy(T.pk[:, 512 * i:512 * i + 512], pt[i][:, 0:512]).then_inc(S["sC%d" % i], 1)

    def v_lc(i):
        V.wait_ge(S.sE0, 1)
        V.wait_ge(S.sE1, 1)
        V.tensor_copy(T.st[:, 0:2], T.lacc[:, 0:2]).then_inc(S.lc, 1)

    def p_pv(i):
        P.wait_ge(S["sC%d" % i], 1)
        for j in range(4):
            P.matmul(ps[i][:, 0:128], T.pk[:, 512 * i + 128 * j:512 * i + 128 * j + 128], vblk(j),
                     j == 0, j == 3 and i < 2).then_inc(S["sO%d" % i], 1)

    def a_ev(i):
        A.wait_ge(S["sO%d" % i], 4)
        A.activation(T.ob[:, 128 * i:128 * i + 128], ps[i][:, 0:128], Copy).then_inc(S["sV%d" % i], 1)

    jn = S.jn

    def v_jd(i):
        V.wait_ge(S["sM%d" % i], 1)
        V.tensor_scalar(T.sm[:, i - 2:i - 1], nmcol(i), T.xs[:, i:i + 1], 30.0, AluOpType.subtract,
                        AluOpType.min).then_inc(jn, 1)

    def v_jg(i):
        V.tensor_scalar(T.dg[:, 128 * (i - 2):128 * (i - 2) + 128], T.ident[:, :], T.sm[:, i:i + 1], None,
                        AluOpType.mult).then_inc(S["sL%d" % i], 1)

    def v_jl(i):
        V.tensor_scalar(T.sm[:, i + 2:i + 3], T.xs[:, i - 2:i - 1], T.sm[:, i:i + 1], T.lacc[:, i:i + 1], AluOpType.mult,
                        AluOpType.add).then_inc(jn, 1)

    def p_jm(i):
        P.wait_ge(S["xa%d" % i], len(eb))
        P.wait_ge(S["sL%d" % i], 1)
        P.matmul(ps[i][:, 0:128], T.dg[:, 128 * (i - 2):128 * (i - 2) + 128], T.xr[:, 128 * (i - 2):128 * (i - 2) + 128],
                 False, True).then_inc(S["sO%d" % i], 1)

    for f, i in ((v_max, 0), (v_max, 1), (v_max, 2), (v_cp, 0), (v_lc, 0), (v_cp, 1), (v_max, 3), (v_cp, 2)):
        f(i)
    V.wait_ge(S.id1, 1)
    V.wait_ge(S.xsa, len(eb))
    v_jd(2)
    v_jd(3)
    V.wait_ge(jn, 3)
    for f, i in ((v_jg, 2), (v_jg, 3), (v_cp, 3), (v_jl, 2), (v_jl, 3)):
        f(i)
    V.wait_ge(jn, 5)
    V.reciprocal(T.sm[:, 6:8], T.sm[:, 4:6]).then_inc(jn, 1)
    V.wait_ge(jn, 6)
    V.wait_ge(S.sO3, 5)
    V.tensor_scalar(T.yb[:, 128:256], ps[3][:, 0:128], T.sm[:, 7:8], None, AluOpType.mult).then_inc(S.sV3, 1)
    for f, i in ((a_exp, 0), (a_exp, 1), (a_exp, 2), (a_ev, 0), (a_ev, 1), (a_exp, 3)):
        f(i)
    A.wait_ge(jn, 2)
    A.activation(T.sm[:, 2:4], T.sm[:, 0:2], Exp).then_inc(jn, 1)
    A.wait_ge(jn, 6)
    A.wait_ge(S.sO2, 5)
    A.activation(T.yb[:, 0:128], ps[2][:, 0:128], Copy, scale=T.sm[:, 6:7]).then_inc(S.sV2, 1)
    P.wait_ge(S.id1, 1)
    for f, i in ((p_tr, 0), (p_tr, 1), (p_pv, 0), (p_pv, 1), (p_tr, 2), (p_tr, 3), (p_pv, 2), (p_jm, 2), (p_pv, 3),
                 (p_jm, 3)):
        f(i)
    rid, pid, _ = topo.addr(far[h])
    g.wait_ge(S.sM0, 1)
    g.wait_ge(S.sM1, 1)
    g.wait_ge(S.lc, 1)
    g.remote_dma(T.xs[:, :], T.st[:, :], S.xsa, S.snt, pid, rid, _join(eb))
    sent += len(eb)
    for i in range(2):
        g.wait_ge(S["sV%d" % i], 1)
        g.remote_dma(T.xr[:, 128 * i:128 * i + 128], T.ob[:, 128 * i:128 * i + 128], S["xa%d" % (i + 2)], S.snt, pid, rid,
                     _join(eb))
        sent += len(eb)
    half = len(eb) // 2
    for a in range(2):
        g.wait_ge(S["sV%d" % (a + 2)], 1)
        trs = []
        for b in range(2):
            rid, pid, _ = topo.addr(cores[cls[p][2 * a + b]])
            trs.append(RemoteDMATransfer(dst_ids=[DstId(rid=rid, pnc=pid)],
                                         dma_engine_mask=_join(eb[half * b:half * b + half]),
                                         remote_sem=S["rs%d" % h], src=T.yb[:, 128 * a:128 * a + 128],
                                         dst=T.res[:, 128 * h:128 * h + 128]))
            sent += half
        g.remote_dma_fused(trs, local_sem=S.snt)
    g.wait_ge(S.snt, sent)


def rank_program(g, core, T, topo):
    cores, cls, work = _plan(T, topo)
    for p in range(2):
        for n in range(NH):
            if cores[cls[p][n]] == core:
                _rank(g, core, T, topo, cores, cls, work, p, n)
            if work[p][n] == core:
                _worker(g, core, T, topo, cores, cls, work, p, n)
